import numpy as np
import ml_dtypes


def mxq(x, axis, fmt="e4m3"):
    dtype, down = {"e4m3": (ml_dtypes.float8_e4m3fn, 7), "e5m2": (ml_dtypes.float8_e5m2, 14)}[fmt]
    v = np.moveaxis(np.asarray(x, np.float32).astype(ml_dtypes.bfloat16).astype(np.float64), axis, -1)
    blocks = v.reshape(v.shape[:-1] + (-1, 32))
    amax = np.abs(blocks).max(-1, keepdims=True)
    byte = np.maximum(np.where(amax > 0, np.frexp(amax)[1] - 1 + 127, 0) - down, 1)
    scale = np.exp2(byte - 127.0)
    codes = (blocks / scale).astype(np.float32).astype(dtype).astype(np.float64)
    return np.moveaxis((codes * scale).reshape(v.shape), -1, axis)


WIDE = False


def mx_kscale(k):
    if not WIDE:
        return np.ones(k)
    levels = np.array([10, -10, 5, -5, 0])
    if k % 512:
        return np.exp2(np.random.permutation(np.resize(levels, k // 32))).repeat(32)
    a = np.empty((k // 512, 16))
    for p in range(k // 512):
        a[p, :8] = np.random.permutation(np.resize(levels, 8))
        for g in range(8):
            far = levels[np.abs(levels - a[p, g]) >= 10]
            a[p, g + 8] = far[np.random.randint(len(far))]
    return np.exp2(a.ravel()).repeat(32)


def f64(x):
    return np.asarray(x).astype(np.float64)


def striped8(idx):
    return np.asarray(idx).reshape(8, -1, 16).transpose(0, 2, 1).reshape(128, -1).astype(np.uint16)


def unstriped8(offs):
    return offs.reshape(8, 16, -1).transpose(0, 2, 1).reshape(8, -1).astype(np.int64)


def pick8(x, idx, run):
    r = np.arange(len(x))
    return x[r[:, None], idx[r % (8 * run) // run]]


E2M1 = np.array([0.0, 0.5, 1.0, 1.5, 2.0, 3.0, 4.0, 6.0, -0.0, -0.5, -1.0, -1.5, -2.0, -3.0, -4.0, -6.0])


def pack_weight(w, fmt):
    k, n = w.shape
    w = f64(np.asarray(w, np.float32).astype(ml_dtypes.bfloat16)).reshape(k // 32, 32, n)
    amax = np.abs(w).max(1)
    if fmt == "e4m3":
        byte = np.frexp(amax)[1] - 1 + 127 - 7
    else:
        mant, ex = np.frexp(amax / 6.0)
        byte = np.where(mant > 0.5, ex, ex - 1) + 127
    byte = np.clip(np.where(amax > 0, byte, 1), 1, 254)
    scaled = (w * np.exp2(127.0 - byte)[:, None, :]).reshape(k, n).astype(np.float32)
    by_word = np.ascontiguousarray(scaled.reshape(k // 512, 128, 4, n).transpose(0, 1, 3, 2))
    if fmt == "e4m3":
        words = by_word.astype(ml_dtypes.float8_e4m3fn).view(np.uint8)
    else:
        c = by_word.astype(ml_dtypes.float4_e2m1fn).view(np.uint8) & 0xF
        words = (c[..., 0::2] | (c[..., 1::2] << 4)).reshape(k // 512, 128, 2 * n)
    return np.ascontiguousarray(words), np.ascontiguousarray(byte.astype(np.uint8).reshape(k // 512, 16, n))


def unpack_weight(words, scales, fmt):
    g, _, n = scales.shape
    words = np.ascontiguousarray(words).reshape(g, 128, n, -1)
    if fmt == "e4m3":
        vals = words.view(ml_dtypes.float8_e4m3fn).astype(np.float64)
    else:
        nib = np.empty((g, 128, n, 4), np.uint8)
        nib[..., 0::2] = words & 0xF
        nib[..., 1::2] = words >> 4
        vals = E2M1[nib]
    vals = vals * np.repeat(np.exp2(scales.astype(np.float64) - 127.0), 8, axis=1)[..., None]
    return vals.transpose(0, 1, 3, 2).reshape(g * 512, n)


D, T, I, Q, E = 512, 1024, 512, 512, 256


def setup_inputs():
    n = np.random.standard_normal
    idx = np.stack([np.random.permutation(T)[:I] for _ in range(8)])
    idx2 = np.stack([np.random.permutation(T)[:I] for _ in range(8)])
    idx3 = np.stack([np.random.permutation(T)[:I] for _ in range(8)])
    idx4 = np.stack([np.random.permutation(T)[:I] for _ in range(8)])
    idx5 = np.stack([np.random.permutation(T)[:I] for _ in range(8)])
    idx6 = np.stack([np.random.permutation(T)[:I] for _ in range(8)])
    fd = mx_kscale(D)
    fq = mx_kscale(Q)
    keysp = pack_weight(n((D, T)) / fd[:, None], "e4m3")
    mixp = pack_weight(n((Q, E)) * 1.0 / np.sqrt(Q) / fq[:, None], "e2m1")
    return {
        "query": (n((D, Q)) * 1.0 / np.sqrt(D) * fd[:, None]).astype(np.float32),
        "keys_words": keysp[0],
        "keys_scales": keysp[1],
        "rowf": (np.random.uniform(0.5, 2.0, (Q, 1)) * fq[:, None]).astype(np.float32),
        "mix_words": mixp[0],
        "mix_scales": mixp[1],
        "offs": striped8(idx),
        "offs2": striped8(idx2),
        "offs3": striped8(idx3),
        "offs4": striped8(idx4),
        "offs5": striped8(idx5),
        "offs6": striped8(idx6),
    }


def reference(query, keys_words, keys_scales, rowf, mix_words, mix_scales, offs, offs2, offs3, offs4, offs5, offs6):
    idx = unstriped8(offs)
    idx2 = unstriped8(offs2)
    idx3 = unstriped8(offs3)
    idx4 = unstriped8(offs4)
    idx5 = unstriped8(offs5)
    idx6 = unstriped8(offs6)
    keysu = unpack_weight(keys_words, keys_scales, "e4m3")
    mixu = unpack_weight(mix_words, mix_scales, "e2m1")
    queryq = mxq(f64(query), 0, "e4m3")
    a = queryq.T @ keysu
    f1 = np.zeros((Q, T))
    f1[np.arange(Q)[:, None], idx2[np.arange(Q) % 512 // 64]] = pick8(a, idx, 64)
    f2 = np.zeros((Q, T))
    f2[np.arange(Q)[:, None], idx4[np.arange(Q) % 512 // 64]] = pick8(a, idx3, 64)
    c1 = a + f1
    c2 = a - f2
    g = np.maximum(pick8(c1, idx5, 64), pick8(c2, idx6, 64))
    gw = g * f64(rowf)
    gwq = mxq(gw, 0, "e4m3")
    y = mixu.T @ gwq
    return y

@@ -1,0 +1,152 @@
+from contextlib import ExitStack
+
+import concourse.mybir as mybir
+
+D, T, I, Q, E = 512, 1024, 512, 512, 256
+FLOPS = 2 * D * Q * T + 2 * Q * E * I
+
+F32 = mybir.dt.float32
+BF16 = mybir.dt.bfloat16
+I32 = mybir.dt.int32
+U32 = mybir.dt.uint32
+U16 = mybir.dt.uint16
+U8 = mybir.dt.uint8
+FP8X4 = mybir.dt.float8_e4m3fn_x4
+FP4X4 = mybir.dt.float4_e2m1fn_x4
+COPY = mybir.ActivationFunctionType.Copy
+ALU = mybir.AluOpType
+
+P = 128
+PACK = 4
+BANK = 512
+HALF = I // 2
+LCOLS = I // 16
+
+
+def tile_attend_braided_one_mixed_kernel(tc, query, keys_words, keys_scales, rowf, mix_words, mix_scales,
+                                          offs, offs2, offs3, offs4, offs5, offs6, out):
+    nc = tc.nc
+    with ExitStack() as ctx:
+        keep = ctx.enter_context(tc.tile_pool(name="keep", bufs=1))
+        psum = ctx.enter_context(tc.psum_pool(name="psum", bufs=1))
+
+        raw = keep.tile([P, PACK, Q], F32, name="raw")
+        nc.sync.dma_start(out=raw[:], in_=query.rearrange("(p j) q -> p j q", j=PACK))
+        k_codes = keep.tile([P, T], U32, name="k_codes", align_bytes=64)
+        nc.sync.dma_start(out=k_codes[:].bitcast(I32), in_=keys_words[0].rearrange("p n r -> p (n r)").bitcast(I32))
+        k_scales = keep.tile([P, T], U8, name="k_scales", align_bytes=64)
+        for quad in range(4):
+            nc.scalar.dma_start(out=k_scales[32 * quad:32 * quad + 4, :].bitcast(I32),
+                              in_=keys_scales[0, 4 * quad:4 * quad + 4, :].bitcast(I32))
+        lists = []
+        for n, src in enumerate((offs, offs2, offs3, offs4, offs5, offs6)):
+            one = keep.tile([P, LCOLS], U16, name="list%d" % n)
+            nc.sync.dma_start(one[:], src)
+            lists.append(one)
+        pick1, put1, pick2, put2, look1, look2 = lists
+        factor = keep.tile([P, PACK], F32, name="factor")
+        nc.sync.dma_start(out=factor[:], in_=rowf.rearrange("(p t) o -> p (t o)", t=PACK))
+        m_codes = keep.tile([P, 2 * E], U8, name="m_codes", align_bytes=64)
+        nc.sync.dma_start(out=m_codes[:], in_=mix_words[0])
+        m_scales = keep.tile([P, E], U8, name="m_scales", align_bytes=64)
+        for quad in range(4):
+            nc.sync.dma_start(out=m_scales[32 * quad:32 * quad + 4, :].bitcast(I32),
+                              in_=mix_scales[0, 4 * quad:4 * quad + 4, :].bitcast(I32))
+
+        f1 = keep.tile([P, T], F32, name="f1")
+        f2 = keep.tile([P, T], F32, name="f2")
+        nc.vector.memset(f1[:], 0.0)
+        nc.vector.memset(f2[:], 0.0)
+
+        dealt = raw[:].rearrange("p j (m t) -> p m t j", t=PACK)
+        q_first = keep.tile([P, P, PACK], BF16, name="q_first", align_bytes=64)
+        q_rest = keep.tile([P, PACK - 1, P, PACK], BF16, name="q_rest", align_bytes=64)
+        q_codes = keep.tile([P, Q], U32, name="q_codes", align_bytes=64)
+        q_scales = keep.tile([P, Q], U8, name="q_scales", align_bytes=64)
+        nc.vector.tensor_copy(out=q_first[:], in_=dealt[:, :, 0, :])
+        nc.vector.quantize_mx(out=q_codes[:, 0:P].bitcast(FP8X4), scales=q_scales[:, 0:P],
+                              in_=q_first[:].rearrange("p m j -> p (m j)"))
+        nc.scalar.copy(out=q_rest[:].rearrange("p t m j -> p m t j"), in_=dealt[:, :, 1:PACK, :])
+        rest_flat = q_rest[:].rearrange("p t m j -> p (t m j)")
+        nc.vector.quantize_mx(out=q_codes[:, P:2 * P].bitcast(FP8X4), scales=q_scales[:, P:2 * P],
+                              in_=rest_flat[:, 0:PACK * P])
+        nc.vector.quantize_mx(out=q_codes[:, 2 * P:].bitcast(FP8X4), scales=q_scales[:, 2 * P:],
+                              in_=rest_flat[:, PACK * P:])
+
+        halves = [slice(h * HALF, (h + 1) * HALF) for h in range(2)]
+        lhalves = [slice(h * LCOLS // 2, (h + 1) * LCOLS // 2) for h in range(2)]
+        woven = [keep.tile([P, HALF, PACK], BF16, name="woven%d" % h, align_bytes=64) for h in range(2)]
+        last = PACK - 1
+
+        def scores(t):
+            a = keep.tile([P, T], F32, name="a%d" % t)
+            for b in range(2):
+                cols = slice(b * BANK, (b + 1) * BANK)
+                acc = psum.tile([P, BANK], F32, name="acc%d_%d" % (t % 2, b))
+                nc.tensor.matmul_mx(out=acc[:], lhsT=q_codes[:, t * P:(t + 1) * P].bitcast(FP8X4),
+                                    lhsT_scale=q_scales[:, t * P:(t + 1) * P],
+                                    rhs=k_codes[:, cols].bitcast(FP8X4), rhs_scale=k_scales[:, cols],
+                                    start=True, stop=True)
+                if t == 0 and b == 1:
+                    nc.vector.tensor_copy(out=a[:, cols], in_=acc[:])
+                else:
+                    nc.scalar.copy(out=a[:, cols], in_=acc[:])
+            return a
+
+        def gather_shared(dst, window, offsets):
+            nc.vector.tensor_copy(dst[:, halves[0]], window[:].indirect(offsets[:, lhalves[0]]))
+            nc.scalar.activation(dst[:, halves[1]], window[:].indirect(offsets[:, lhalves[1]]), COPY)
+
+        for t in range(PACK):
+            a = scores(t)
+            p1 = keep.tile([P, I], F32, name="p1_%d" % t)
+            p2 = keep.tile([P, I], F32, name="p2_%d" % t)
+            if t == 0:
+                gather_shared(p1, a, pick1)
+            else:
+                nc.scalar.activation(p1[:], a[:].indirect(pick1[:]), COPY)
+            nc.scalar.activation(p2[:], a[:].indirect(pick2[:]), COPY)
+            c1 = keep.tile([P, T], F32, name="c1_%d" % t)
+            c2 = keep.tile([P, T], F32, name="c2_%d" % t)
+            nc.vector.tensor_copy(f1[:].indirect(put1[:]), p1[:])
+            nc.gpsimd.tensor_tensor(c1[:], a[:], f1[:], ALU.add)
+            nc.vector.tensor_copy(f2[:].indirect(put2[:]), p2[:])
+            g1 = keep.tile([P, I], F32, name="g1_%d" % t)
+            g2 = keep.tile([P, I], F32, name="g2_%d" % t)
+            if t < last:
+                g = keep.tile([P, I], F32, name="g_%d" % t)
+            nc.scalar.activation(g1[:], c1[:].indirect(look1[:]), COPY)
+            if t < last:
+                nc.gpsimd.tensor_tensor(c2[:], a[:], f2[:], ALU.subtract)
+                nc.scalar.activation(g2[:], c2[:].indirect(look2[:]), COPY)
+                nc.vector.tensor_tensor(g[:], g1[:], g2[:], ALU.max)
+            else:
+                nc.vector.tensor_tensor(c2[:], a[:], f2[:], ALU.subtract)
+                gather_shared(g2, c2, look2)
+                for h in range(2):
+                    nc.vector.tensor_tensor(g[:, halves[h]], g1[:, halves[h]], g2[:, halves[h]], ALU.max)
+            for h in range(2):
+                if t == last and h == 0:
+                    nc.vector.tensor_scalar(out=woven[h][:, :, t], in0=g[:, halves[h]], scalar1=factor[:, t:t + 1],
+                                            scalar2=None, op0=ALU.mult)
+                else:
+                    nc.scalar.activation(woven[h][:, :, t], g[:, halves[h]], COPY, scale=factor[:, t:t + 1])
+
+        out_view = out.rearrange("(c p) i -> p c i", p=P)
+        for h in range(2):
+            g_codes = keep.tile([P, HALF], U32, name="g_codes%d" % h, align_bytes=64)
+            g_scales = keep.tile([P, HALF], U8, name="g_scales%d" % h, align_bytes=64)
+            nc.vector.quantize_mx(out=g_codes[:].bitcast(FP8X4), scales=g_scales[:],
+                                  in_=woven[h][:].rearrange("p i t -> p (i t)"))
+            res = keep.tile([P, 2, HALF], F32, name="res%d" % h)
+            for c in range(2):
+                acc = psum.tile([P, BANK], F32, name="y%d_%d" % (h, c))
+                nc.tensor.matmul_mx(out=acc[:, 0:HALF], lhsT=m_codes[:, 2 * P * c:2 * P * (c + 1)].bitcast(FP4X4),
+                                    lhsT_scale=m_scales[:, P * c:P * (c + 1)],
+                                    rhs=g_codes[:].bitcast(FP8X4), rhs_scale=g_scales[:],
+                                    start=True, stop=True)
+                if h == 1 and c == 1:
+                    nc.vector.tensor_copy(out=res[:, c, :], in_=acc[:, 0:HALF])
+                else:
+                    nc.scalar.copy(out=res[:, c, :], in_=acc[:, 0:HALF])
+            nc.sync.dma_start(out=out_view[:, :, halves[h]], in_=res[:])

@@ -21,6 +21,7 @@ PACK = 4
 BANK = 512
 HALF = I // 2
 LCOLS = I // 16
+SPLIT = 704
 
 
 def tile_attend_braided_one_mixed_kernel(tc, query, keys_words, keys_scales, rowf, mix_words, mix_scales,
@@ -30,8 +31,10 @@ def tile_attend_braided_one_mixed_kernel(tc, query, keys_words, keys_scales, row
         keep = ctx.enter_context(tc.tile_pool(name="keep", bufs=1))
         psum = ctx.enter_context(tc.psum_pool(name="psum", bufs=1))
 
-        raw = keep.tile([P, PACK, Q], F32, name="raw")
-        nc.sync.dma_start(out=raw[:], in_=query.rearrange("(p j) q -> p j q", j=PACK))
+        raw = [keep.tile([P, PACK, Q // 2], F32, name="raw%d" % u) for u in range(2)]
+        by_partition = query.rearrange("(p j) q -> p j q", j=PACK)
+        for u in range(2):
+            nc.sync.dma_start(out=raw[u][:], in_=by_partition[:, :, u * Q // 2:(u + 1) * Q // 2])
         k_codes = keep.tile([P, T], U32, name="k_codes", align_bytes=64)
         nc.sync.dma_start(out=k_codes[:].bitcast(I32), in_=keys_words[0].rearrange("p n r -> p (n r)").bitcast(I32))
         k_scales = keep.tile([P, T], U8, name="k_scales", align_bytes=64)
@@ -58,15 +61,18 @@ def tile_attend_braided_one_mixed_kernel(tc, query, keys_words, keys_scales, row
         nc.vector.memset(f1[:], 0.0)
         nc.vector.memset(f2[:], 0.0)
 
-        dealt = raw[:].rearrange("p j (m t) -> p m t j", t=PACK)
+        dealt = [raw[u][:].rearrange("p j (m t) -> p m t j", t=PACK) for u in range(2)]
+        rows = [slice(u * P // 2, (u + 1) * P // 2) for u in range(2)]
         q_first = keep.tile([P, P, PACK], BF16, name="q_first", align_bytes=64)
         q_rest = keep.tile([P, PACK - 1, P, PACK], BF16, name="q_rest", align_bytes=64)
         q_codes = keep.tile([P, Q], U32, name="q_codes", align_bytes=64)
         q_scales = keep.tile([P, Q], U8, name="q_scales", align_bytes=64)
-        nc.vector.tensor_copy(out=q_first[:], in_=dealt[:, :, 0, :])
+        for u in range(2):
+            nc.vector.tensor_copy(out=q_first[:, rows[u], :], in_=dealt[u][:, :, 0, :])
         nc.vector.quantize_mx(out=q_codes[:, 0:P].bitcast(FP8X4), scales=q_scales[:, 0:P],
                               in_=q_first[:].rearrange("p m j -> p (m j)"))
-        nc.scalar.copy(out=q_rest[:].rearrange("p t m j -> p m t j"), in_=dealt[:, :, 1:PACK, :])
+        for u in range(2):
+            nc.scalar.copy(out=q_rest[:].rearrange("p t m j -> p m t j")[:, rows[u], :, :], in_=dealt[u][:, :, 1:PACK, :])
         rest_flat = q_rest[:].rearrange("p t m j -> p (t m j)")
         nc.vector.quantize_mx(out=q_codes[:, P:2 * P].bitcast(FP8X4), scales=q_scales[:, P:2 * P],
                               in_=rest_flat[:, 0:PACK * P])
@@ -78,75 +84,123 @@ def tile_attend_braided_one_mixed_kernel(tc, query, keys_words, keys_scales, row
         woven = [keep.tile([P, HALF, PACK], BF16, name="woven%d" % h, align_bytes=64) for h in range(2)]
         last = PACK - 1
 
+        banks = {}
+
         def scores(t):
-            a = keep.tile([P, T], F32, name="a%d" % t)
-            for b in range(2):
-                cols = slice(b * BANK, (b + 1) * BANK)
-                acc = psum.tile([P, BANK], F32, name="acc%d_%d" % (t % 2, b))
-                nc.tensor.matmul_mx(out=acc[:], lhsT=q_codes[:, t * P:(t + 1) * P].bitcast(FP8X4),
+            tile_a = keep.tile([P, T], F32, name="a%d" % t)
+            width = BANK // 2 if t == 0 else BANK
+            for b in range(T // width):
+                cols = slice(b * width, (b + 1) * width)
+                acc = psum.tile([P, BANK], F32, name="bank%d" % ((len(banks)) % 8))
+                banks[t, b] = acc
+                nc.tensor.matmul_mx(out=acc[:, 0:width], lhsT=q_codes[:, t * P:(t + 1) * P].bitcast(FP8X4),
                                     lhsT_scale=q_scales[:, t * P:(t + 1) * P],
                                     rhs=k_codes[:, cols].bitcast(FP8X4), rhs_scale=k_scales[:, cols],
                                     start=True, stop=True)
-                if t == 0 and b == 1:
-                    nc.vector.tensor_copy(out=a[:, cols], in_=acc[:])
+                if t == 0 and b % 2 == 1:
+                    nc.vector.tensor_copy(out=tile_a[:, cols], in_=acc[:, 0:width])
                 else:
-                    nc.scalar.copy(out=a[:, cols], in_=acc[:])
-            return a
+                    nc.scalar.copy(out=tile_a[:, cols], in_=acc[:, 0:width])
+            return tile_a
 
         def gather_shared(dst, window, offsets):
             nc.vector.tensor_copy(dst[:, halves[0]], window[:].indirect(offsets[:, lhalves[0]]))
             nc.scalar.activation(dst[:, halves[1]], window[:].indirect(offsets[:, lhalves[1]]), COPY)
 
-        for t in range(PACK):
-            a = scores(t)
-            p1 = keep.tile([P, I], F32, name="p1_%d" % t)
-            p2 = keep.tile([P, I], F32, name="p2_%d" % t)
-            if t == 0:
-                gather_shared(p1, a, pick1)
-            else:
-                nc.scalar.activation(p1[:], a[:].indirect(pick1[:]), COPY)
-            nc.scalar.activation(p2[:], a[:].indirect(pick2[:]), COPY)
-            c1 = keep.tile([P, T], F32, name="c1_%d" % t)
-            c2 = keep.tile([P, T], F32, name="c2_%d" % t)
-            nc.vector.tensor_copy(f1[:].indirect(put1[:]), p1[:])
-            nc.gpsimd.tensor_tensor(c1[:], a[:], f1[:], ALU.add)
-            nc.vector.tensor_copy(f2[:].indirect(put2[:]), p2[:])
-            g1 = keep.tile([P, I], F32, name="g1_%d" % t)
-            g2 = keep.tile([P, I], F32, name="g2_%d" % t)
-            if t < last:
-                g = keep.tile([P, I], F32, name="g_%d" % t)
-            nc.scalar.activation(g1[:], c1[:].indirect(look1[:]), COPY)
-            if t < last:
-                nc.gpsimd.tensor_tensor(c2[:], a[:], f2[:], ALU.subtract)
-                nc.scalar.activation(g2[:], c2[:].indirect(look2[:]), COPY)
-                nc.vector.tensor_tensor(g[:], g1[:], g2[:], ALU.max)
-            else:
-                nc.vector.tensor_tensor(c2[:], a[:], f2[:], ALU.subtract)
-                gather_shared(g2, c2, look2)
-                for h in range(2):
-                    nc.vector.tensor_tensor(g[:, halves[h]], g1[:, halves[h]], g2[:, halves[h]], ALU.max)
-            for h in range(2):
-                if t == last and h == 0:
-                    nc.vector.tensor_scalar(out=woven[h][:, :, t], in0=g[:, halves[h]], scalar1=factor[:, t:t + 1],
-                                            scalar2=None, op0=ALU.mult)
-                else:
-                    nc.scalar.activation(woven[h][:, :, t], g[:, halves[h]], COPY, scale=factor[:, t:t + 1])
+        def tiles(name, width):
+            return [keep.tile([P, width], F32, name="%s_%d" % (name, t)) for t in range(PACK)]
 
-        out_view = out.rearrange("(c p) i -> p c i", p=P)
+        p1, p2, g1, g2 = tiles("p1", I), tiles("p2", I), tiles("g1", I), tiles("g2", I)
+        c1, c2 = tiles("c1", T), tiles("c2", T)
+        larger = [p1[0], p1[1], p2[3], p1[3]]
+        a = {}
+
+        def pick_first(t):
+            if t == 0:
+                gather_shared(p1[t], a[t], pick1)
+            else:
+                nc.scalar.activation(p1[t][:], a[t][:].indirect(pick1[:]), COPY)
+
+        def pick_second(t):
+            nc.scalar.activation(p2[t][:], a[t][:].indirect(pick2[:]), COPY)
+
+        def add_side(t):
+            nc.vector.tensor_copy(f1[:].indirect(put1[:]), p1[t][:])
+            nc.gpsimd.tensor_tensor(c1[t][:], a[t][:], f1[:], ALU.add)
+
+        def subtract_side(t):
+            nc.vector.tensor_copy(f2[:].indirect(put2[:]), p2[t][:])
+            if t < last:
+                nc.gpsimd.tensor_tensor(c2[t][:], a[t][:], f2[:], ALU.subtract)
+            else:
+                nc.vector.tensor_tensor(c2[t][:, 0:BANK], banks[t, 0][:], f2[:, 0:BANK], ALU.subtract)
+                nc.vector.tensor_tensor(c2[t][:, BANK:SPLIT], banks[t, 1][:, 0:SPLIT - BANK], f2[:, BANK:SPLIT], ALU.subtract)
+                nc.gpsimd.tensor_tensor(c2[t][:, SPLIT:], a[t][:, SPLIT:], f2[:, SPLIT:], ALU.subtract)
+
+        def look_first(t):
+            nc.scalar.activation(g1[t][:], c1[t][:].indirect(look1[:]), COPY)
+
+        def look_second(t):
+            nc.scalar.activation(g2[t][:], c2[t][:].indirect(look2[:]), COPY)
+
+        def take_larger(t):
+            parts = halves if t == last else [slice(0, I)]
+            for cols in parts:
+                nc.vector.tensor_tensor(larger[t][:, cols], g1[t][:, cols], g2[t][:, cols], ALU.max)
+
+        def weave(t):
+            for h in range(2):
+                if t >= 2:
+                    nc.vector.tensor_scalar(out=woven[h][:, :, t], in0=larger[t][:, halves[h]],
+                                            scalar1=factor[:, t:t + 1], scalar2=None, op0=ALU.mult)
+                else:
+                    nc.scalar.activation(woven[h][:, :, t], larger[t][:, halves[h]], COPY, scale=factor[:, t:t + 1])
+
+        for t in range(2):
+            a[t] = scores(t)
+            pick_first(t)
+            pick_second(t)
+            add_side(t)
+            subtract_side(t)
+        for t in range(2, PACK):
+            if t == 2:
+                a[t] = scores(t)
+            look_first(t - 2)
+            if t == 3:
+                weave(0)
+            look_second(t - 2)
+            take_larger(t - 2)
+            pick_first(t)
+            pick_second(t)
+            if t == 2:
+                a[3] = scores(3)
+            add_side(t)
+            subtract_side(t)
+        look_first(2)
+        weave(1)
+        look_second(2)
+        take_larger(2)
+        weave(2)
+        look_first(3)
+        look_second(3)
+        take_larger(3)
+        weave(3)
+
         for h in range(2):
             g_codes = keep.tile([P, HALF], U32, name="g_codes%d" % h, align_bytes=64)
             g_scales = keep.tile([P, HALF], U8, name="g_scales%d" % h, align_bytes=64)
             nc.vector.quantize_mx(out=g_codes[:].bitcast(FP8X4), scales=g_scales[:],
                                   in_=woven[h][:].rearrange("p i t -> p (i t)"))
-            res = keep.tile([P, 2, HALF], F32, name="res%d" % h)
             for c in range(2):
-                acc = psum.tile([P, BANK], F32, name="y%d_%d" % (h, c))
+                res = keep.tile([P, HALF], F32, name="res%d_%d" % (h, c))
+                acc = psum.tile([P, BANK], F32, name="bank%d" % (2 + 2 * h + c))
                 nc.tensor.matmul_mx(out=acc[:, 0:HALF], lhsT=m_codes[:, 2 * P * c:2 * P * (c + 1)].bitcast(FP4X4),
                                     lhsT_scale=m_scales[:, P * c:P * (c + 1)],
                                     rhs=g_codes[:].bitcast(FP8X4), rhs_scale=g_scales[:],
                                     start=True, stop=True)
                 if h == 1 and c == 1:
-                    nc.vector.tensor_copy(out=res[:, c, :], in_=acc[:, 0:HALF])
+                    nc.vector.tensor_copy(out=res[:], in_=acc[:, 0:HALF])
                 else:
-                    nc.scalar.copy(out=res[:, c, :], in_=acc[:, 0:HALF])
-            nc.sync.dma_start(out=out_view[:, :, halves[h]], in_=res[:])
+                    nc.scalar.copy(out=res[:], in_=acc[:, 0:HALF])
+                queue = nc.scalar if (h == 1 and c == 0) else nc.sync
+                queue.dma_start(out=out[c * P:(c + 1) * P, halves[h]], in_=res[:])

@@ -18,10 +18,13 @@ ALU = mybir.AluOpType
 
 P = 128
 PACK = 4
+LAST = PACK - 1
 BANK = 512
+BANKS = 8
 HALF = I // 2
-LCOLS = I // 16
-SPLIT = 704
+LIST_COLS = I // 16
+SPLIT = 768
+FIRST_OUT_BANK = 2
 
 
 def tile_attend_braided_one_mixed_kernel(tc, query, keys_words, keys_scales, rowf, mix_words, mix_scales,
@@ -31,19 +34,22 @@ def tile_attend_braided_one_mixed_kernel(tc, query, keys_words, keys_scales, row
         keep = ctx.enter_context(tc.tile_pool(name="keep", bufs=1))
         psum = ctx.enter_context(tc.psum_pool(name="psum", bufs=1))
 
-        raw = [keep.tile([P, PACK, Q // 2], F32, name="raw%d" % u) for u in range(2)]
-        by_partition = query.rearrange("(p j) q -> p j q", j=PACK)
+        raw = keep.tile([P, PACK * Q], F32, name="raw")
+        by_partition = query.rearrange("(p j) q -> p (j q)", j=PACK)
         for u in range(2):
-            nc.sync.dma_start(out=raw[u][:], in_=by_partition[:, :, u * Q // 2:(u + 1) * Q // 2])
+            nc.sync.dma_start(out=raw[:, 2 * Q * u:2 * Q * (u + 1)], in_=by_partition[:, 2 * Q * u:2 * Q * (u + 1)])
         k_codes = keep.tile([P, T], U32, name="k_codes", align_bytes=64)
-        nc.sync.dma_start(out=k_codes[:].bitcast(I32), in_=keys_words[0].rearrange("p n r -> p (n r)").bitcast(I32))
+        key_words = keys_words[0].rearrange("p n r -> p (n r)").bitcast(I32)
+        for u in range(2):
+            nc.sync.dma_start(out=k_codes[:, u * BANK:(u + 1) * BANK].bitcast(I32),
+                              in_=key_words[:, u * BANK:(u + 1) * BANK])
         k_scales = keep.tile([P, T], U8, name="k_scales", align_bytes=64)
         for quad in range(4):
             nc.scalar.dma_start(out=k_scales[32 * quad:32 * quad + 4, :].bitcast(I32),
-                              in_=keys_scales[0, 4 * quad:4 * quad + 4, :].bitcast(I32))
+                                in_=keys_scales[0, 4 * quad:4 * quad + 4, :].bitcast(I32))
         lists = []
         for n, src in enumerate((offs, offs2, offs3, offs4, offs5, offs6)):
-            one = keep.tile([P, LCOLS], U16, name="list%d" % n)
+            one = keep.tile([P, LIST_COLS], U16, name="list%d" % n)
             nc.sync.dma_start(one[:], src)
             lists.append(one)
         pick1, put1, pick2, put2, look1, look2 = lists
@@ -61,18 +67,18 @@ def tile_attend_braided_one_mixed_kernel(tc, query, keys_words, keys_scales, row
         nc.vector.memset(f1[:], 0.0)
         nc.vector.memset(f2[:], 0.0)
 
-        dealt = [raw[u][:].rearrange("p j (m t) -> p m t j", t=PACK) for u in range(2)]
-        rows = [slice(u * P // 2, (u + 1) * P // 2) for u in range(2)]
         q_first = keep.tile([P, P, PACK], BF16, name="q_first", align_bytes=64)
         q_rest = keep.tile([P, PACK - 1, P, PACK], BF16, name="q_rest", align_bytes=64)
         q_codes = keep.tile([P, Q], U32, name="q_codes", align_bytes=64)
         q_scales = keep.tile([P, Q], U8, name="q_scales", align_bytes=64)
         for u in range(2):
-            nc.vector.tensor_copy(out=q_first[:, rows[u], :], in_=dealt[u][:, :, 0, :])
+            pair = raw[:, 2 * Q * u:2 * Q * (u + 1)].rearrange("p (j m t) -> p m t j", j=2, t=PACK)
+            cast = nc.scalar.copy if u == 0 else nc.vector.tensor_copy
+            cast(out=q_first[:, :, 2 * u:2 * u + 2], in_=pair[:, :, 0, :])
         nc.vector.quantize_mx(out=q_codes[:, 0:P].bitcast(FP8X4), scales=q_scales[:, 0:P],
                               in_=q_first[:].rearrange("p m j -> p (m j)"))
-        for u in range(2):
-            nc.scalar.copy(out=q_rest[:].rearrange("p t m j -> p m t j")[:, rows[u], :, :], in_=dealt[u][:, :, 1:PACK, :])
+        dealt = raw[:].rearrange("p (j m t) -> p m t j", j=PACK, t=PACK)
+        nc.scalar.copy(out=q_rest[:].rearrange("p t m j -> p m t j"), in_=dealt[:, :, 1:PACK, :])
         rest_flat = q_rest[:].rearrange("p t m j -> p (t m j)")
         nc.vector.quantize_mx(out=q_codes[:, P:2 * P].bitcast(FP8X4), scales=q_scales[:, P:2 * P],
                               in_=rest_flat[:, 0:PACK * P])
@@ -80,44 +86,36 @@ def tile_attend_braided_one_mixed_kernel(tc, query, keys_words, keys_scales, row
                               in_=rest_flat[:, PACK * P:])
 
         halves = [slice(h * HALF, (h + 1) * HALF) for h in range(2)]
-        lhalves = [slice(h * LCOLS // 2, (h + 1) * LCOLS // 2) for h in range(2)]
+        list_halves = [slice(h * LIST_COLS // 2, (h + 1) * LIST_COLS // 2) for h in range(2)]
         woven = [keep.tile([P, HALF, PACK], BF16, name="woven%d" % h, align_bytes=64) for h in range(2)]
-        last = PACK - 1
-
         banks = {}
 
+        def tiles(name, width):
+            return [keep.tile([P, width], F32, name="%s_%d" % (name, t)) for t in range(PACK)]
+
+        a, c1, c2 = tiles("a", T), tiles("c1", T), tiles("c2", T)
+        p1, p2, g1, g2 = tiles("p1", I), tiles("p2", I), tiles("g1", I), tiles("g2", I)
+        larger = [p1[0], p1[1], p2[LAST], p1[LAST]]
+
         def scores(t):
-            tile_a = keep.tile([P, T], F32, name="a%d" % t)
             width = BANK // 2 if t == 0 else BANK
             for b in range(T // width):
                 cols = slice(b * width, (b + 1) * width)
-                acc = psum.tile([P, BANK], F32, name="bank%d" % ((len(banks)) % 8))
+                acc = psum.tile([P, BANK], F32, name="bank%d" % (len(banks) % BANKS))
                 banks[t, b] = acc
                 nc.tensor.matmul_mx(out=acc[:, 0:width], lhsT=q_codes[:, t * P:(t + 1) * P].bitcast(FP8X4),
                                     lhsT_scale=q_scales[:, t * P:(t + 1) * P],
                                     rhs=k_codes[:, cols].bitcast(FP8X4), rhs_scale=k_scales[:, cols],
                                     start=True, stop=True)
                 if t == 0 and b % 2 == 1:
-                    nc.vector.tensor_copy(out=tile_a[:, cols], in_=acc[:, 0:width])
+                    nc.vector.tensor_copy(out=a[t][:, cols], in_=acc[:, 0:width])
                 else:
-                    nc.scalar.copy(out=tile_a[:, cols], in_=acc[:, 0:width])
-            return tile_a
-
-        def gather_shared(dst, window, offsets):
-            nc.vector.tensor_copy(dst[:, halves[0]], window[:].indirect(offsets[:, lhalves[0]]))
-            nc.scalar.activation(dst[:, halves[1]], window[:].indirect(offsets[:, lhalves[1]]), COPY)
-
-        def tiles(name, width):
-            return [keep.tile([P, width], F32, name="%s_%d" % (name, t)) for t in range(PACK)]
-
-        p1, p2, g1, g2 = tiles("p1", I), tiles("p2", I), tiles("g1", I), tiles("g2", I)
-        c1, c2 = tiles("c1", T), tiles("c2", T)
-        larger = [p1[0], p1[1], p2[3], p1[3]]
-        a = {}
+                    nc.scalar.copy(out=a[t][:, cols], in_=acc[:, 0:width])
 
         def pick_first(t):
             if t == 0:
-                gather_shared(p1[t], a[t], pick1)
+                nc.vector.tensor_copy(p1[t][:, halves[0]], a[t][:].indirect(pick1[:, list_halves[0]]))
+                nc.scalar.activation(p1[t][:, halves[1]], a[t][:].indirect(pick1[:, list_halves[1]]), COPY)
             else:
                 nc.scalar.activation(p1[t][:], a[t][:].indirect(pick1[:]), COPY)
 
@@ -130,11 +128,12 @@ def tile_attend_braided_one_mixed_kernel(tc, query, keys_words, keys_scales, row
 
         def subtract_side(t):
             nc.vector.tensor_copy(f2[:].indirect(put2[:]), p2[t][:])
-            if t < last:
+            if t < LAST:
                 nc.gpsimd.tensor_tensor(c2[t][:], a[t][:], f2[:], ALU.subtract)
             else:
                 nc.vector.tensor_tensor(c2[t][:, 0:BANK], banks[t, 0][:], f2[:, 0:BANK], ALU.subtract)
-                nc.vector.tensor_tensor(c2[t][:, BANK:SPLIT], banks[t, 1][:, 0:SPLIT - BANK], f2[:, BANK:SPLIT], ALU.subtract)
+                nc.vector.tensor_tensor(c2[t][:, BANK:SPLIT], banks[t, 1][:, 0:SPLIT - BANK], f2[:, BANK:SPLIT],
+                                        ALU.subtract)
                 nc.gpsimd.tensor_tensor(c2[t][:, SPLIT:], a[t][:, SPLIT:], f2[:, SPLIT:], ALU.subtract)
 
         def look_first(t):
@@ -144,56 +143,26 @@ def tile_attend_braided_one_mixed_kernel(tc, query, keys_words, keys_scales, row
             nc.scalar.activation(g2[t][:], c2[t][:].indirect(look2[:]), COPY)
 
         def take_larger(t):
-            parts = halves if t == last else [slice(0, I)]
+            parts = halves if t == LAST else [slice(0, I)]
             for cols in parts:
                 nc.vector.tensor_tensor(larger[t][:, cols], g1[t][:, cols], g2[t][:, cols], ALU.max)
 
         def weave(t):
             for h in range(2):
-                if t >= 2:
+                if t >= PACK // 2:
                     nc.vector.tensor_scalar(out=woven[h][:, :, t], in0=larger[t][:, halves[h]],
                                             scalar1=factor[:, t:t + 1], scalar2=None, op0=ALU.mult)
                 else:
                     nc.scalar.activation(woven[h][:, :, t], larger[t][:, halves[h]], COPY, scale=factor[:, t:t + 1])
 
-        for t in range(2):
-            a[t] = scores(t)
-            pick_first(t)
-            pick_second(t)
-            add_side(t)
-            subtract_side(t)
-        for t in range(2, PACK):
-            if t == 2:
-                a[t] = scores(t)
-            look_first(t - 2)
-            if t == 3:
-                weave(0)
-            look_second(t - 2)
-            take_larger(t - 2)
-            pick_first(t)
-            pick_second(t)
-            if t == 2:
-                a[3] = scores(3)
-            add_side(t)
-            subtract_side(t)
-        look_first(2)
-        weave(1)
-        look_second(2)
-        take_larger(2)
-        weave(2)
-        look_first(3)
-        look_second(3)
-        take_larger(3)
-        weave(3)
-
-        for h in range(2):
+        def mix_half(h):
             g_codes = keep.tile([P, HALF], U32, name="g_codes%d" % h, align_bytes=64)
             g_scales = keep.tile([P, HALF], U8, name="g_scales%d" % h, align_bytes=64)
             nc.vector.quantize_mx(out=g_codes[:].bitcast(FP8X4), scales=g_scales[:],
                                   in_=woven[h][:].rearrange("p i t -> p (i t)"))
-            for c in range(2):
+            for c in range(E // P):
                 res = keep.tile([P, HALF], F32, name="res%d_%d" % (h, c))
-                acc = psum.tile([P, BANK], F32, name="bank%d" % (2 + 2 * h + c))
+                acc = psum.tile([P, BANK], F32, name="bank%d" % (FIRST_OUT_BANK + 2 * h + c))
                 nc.tensor.matmul_mx(out=acc[:, 0:HALF], lhsT=m_codes[:, 2 * P * c:2 * P * (c + 1)].bitcast(FP4X4),
                                     lhsT_scale=m_scales[:, P * c:P * (c + 1)],
                                     rhs=g_codes[:].bitcast(FP8X4), rhs_scale=g_scales[:],
@@ -204,3 +173,38 @@ def tile_attend_braided_one_mixed_kernel(tc, query, keys_words, keys_scales, row
                     nc.scalar.copy(out=res[:], in_=acc[:, 0:HALF])
                 queue = nc.scalar if (h == 1 and c == 0) else nc.sync
                 queue.dma_start(out=out[c * P:(c + 1) * P, halves[h]], in_=res[:])
+
+        for t in range(2):
+            scores(t)
+            pick_first(t)
+            pick_second(t)
+            add_side(t)
+            subtract_side(t)
+        scores(2)
+        look_first(0)
+        look_second(0)
+        take_larger(0)
+        pick_first(2)
+        pick_second(2)
+        scores(3)
+        add_side(2)
+        subtract_side(2)
+        look_first(1)
+        weave(0)
+        look_second(1)
+        take_larger(1)
+        pick_first(3)
+        pick_second(3)
+        add_side(3)
+        subtract_side(3)
+        look_first(2)
+        weave(1)
+        look_second(2)
+        take_larger(2)
+        weave(2)
+        look_first(3)
+        look_second(3)
+        take_larger(3)
+        weave(3)
+        for h in range(2):
+            mix_half(h)

from contextlib import ExitStack

import concourse.mybir as mybir

D, T, I, Q, E = 512, 1024, 512, 512, 256
FLOPS = 2 * D * Q * T + 2 * Q * E * I

F32 = mybir.dt.float32
BF16 = mybir.dt.bfloat16
I32 = mybir.dt.int32
U32 = mybir.dt.uint32
U16 = mybir.dt.uint16
U8 = mybir.dt.uint8
FP8X4 = mybir.dt.float8_e4m3fn_x4
FP4X4 = mybir.dt.float4_e2m1fn_x4
COPY = mybir.ActivationFunctionType.Copy
ALU = mybir.AluOpType

P = 128
PACK = 4
LAST = PACK - 1
BANK = 512
BANKS = 8
HALF = I // 2
LIST_COLS = I // 16
SPLIT = 768
FIRST_OUT_BANK = 2


def tile_attend_braided_one_mixed_kernel(tc, query, keys_words, keys_scales, rowf, mix_words, mix_scales,
                                          offs, offs2, offs3, offs4, offs5, offs6, out):
    nc = tc.nc
    with ExitStack() as ctx:
        keep = ctx.enter_context(tc.tile_pool(name="keep", bufs=1))
        psum = ctx.enter_context(tc.psum_pool(name="psum", bufs=1))

        raw = keep.tile([P, PACK * Q], F32, name="raw")
        by_partition = query.rearrange("(p j) q -> p (j q)", j=PACK)
        for u in range(2):
            nc.sync.dma_start(out=raw[:, 2 * Q * u:2 * Q * (u + 1)], in_=by_partition[:, 2 * Q * u:2 * Q * (u + 1)])
        k_codes = keep.tile([P, T], U32, name="k_codes", align_bytes=64)
        key_words = keys_words[0].rearrange("p n r -> p (n r)").bitcast(I32)
        for u in range(2):
            nc.sync.dma_start(out=k_codes[:, u * BANK:(u + 1) * BANK].bitcast(I32),
                              in_=key_words[:, u * BANK:(u + 1) * BANK])
        k_scales = keep.tile([P, T], U8, name="k_scales", align_bytes=64)
        for quad in range(4):
            nc.scalar.dma_start(out=k_scales[32 * quad:32 * quad + 4, :].bitcast(I32),
                                in_=keys_scales[0, 4 * quad:4 * quad + 4, :].bitcast(I32))
        lists = []
        for n, src in enumerate((offs, offs2, offs3, offs4, offs5, offs6)):
            one = keep.tile([P, LIST_COLS], U16, name="list%d" % n)
            nc.sync.dma_start(one[:], src)
            lists.append(one)
        pick1, put1, pick2, put2, look1, look2 = lists
        factor = keep.tile([P, PACK], F32, name="factor")
        nc.sync.dma_start(out=factor[:], in_=rowf.rearrange("(p t) o -> p (t o)", t=PACK))
        m_codes = keep.tile([P, 2 * E], U8, name="m_codes", align_bytes=64)
        nc.sync.dma_start(out=m_codes[:], in_=mix_words[0])
        m_scales = keep.tile([P, E], U8, name="m_scales", align_bytes=64)
        for quad in range(4):
            nc.sync.dma_start(out=m_scales[32 * quad:32 * quad + 4, :].bitcast(I32),
                              in_=mix_scales[0, 4 * quad:4 * quad + 4, :].bitcast(I32))

        f1 = keep.tile([P, T], F32, name="f1")
        f2 = keep.tile([P, T], F32, name="f2")
        nc.vector.memset(f1[:], 0.0)
        nc.vector.memset(f2[:], 0.0)

        q_first = keep.tile([P, P, PACK], BF16, name="q_first", align_bytes=64)
        q_rest = keep.tile([P, PACK - 1, P, PACK], BF16, name="q_rest", align_bytes=64)
        q_codes = keep.tile([P, Q], U32, name="q_codes", align_bytes=64)
        q_scales = keep.tile([P, Q], U8, name="q_scales", align_bytes=64)
        for u in range(2):
            pair = raw[:, 2 * Q * u:2 * Q * (u + 1)].rearrange("p (j m t) -> p m t j", j=2, t=PACK)
            cast = nc.scalar.copy if u == 0 else nc.vector.tensor_copy
            cast(out=q_first[:, :, 2 * u:2 * u + 2], in_=pair[:, :, 0, :])
        nc.vector.quantize_mx(out=q_codes[:, 0:P].bitcast(FP8X4), scales=q_scales[:, 0:P],
                              in_=q_first[:].rearrange("p m j -> p (m j)"))
        dealt = raw[:].rearrange("p (j m t) -> p m t j", j=PACK, t=PACK)
        nc.scalar.copy(out=q_rest[:].rearrange("p t m j -> p m t j"), in_=dealt[:, :, 1:PACK, :])
        rest_flat = q_rest[:].rearrange("p t m j -> p (t m j)")
        nc.vector.quantize_mx(out=q_codes[:, P:2 * P].bitcast(FP8X4), scales=q_scales[:, P:2 * P],
                              in_=rest_flat[:, 0:PACK * P])
        nc.vector.quantize_mx(out=q_codes[:, 2 * P:].bitcast(FP8X4), scales=q_scales[:, 2 * P:],
                              in_=rest_flat[:, PACK * P:])

        halves = [slice(h * HALF, (h + 1) * HALF) for h in range(2)]
        list_halves = [slice(h * LIST_COLS // 2, (h + 1) * LIST_COLS // 2) for h in range(2)]
        woven = [keep.tile([P, HALF, PACK], BF16, name="woven%d" % h, align_bytes=64) for h in range(2)]
        banks = {}

        def tiles(name, width):
            return [keep.tile([P, width], F32, name="%s_%d" % (name, t)) for t in range(PACK)]

        a, c1, c2 = tiles("a", T), tiles("c1", T), tiles("c2", T)
        p1, p2, g1, g2 = tiles("p1", I), tiles("p2", I), tiles("g1", I), tiles("g2", I)
        larger = [p1[0], p1[1], p2[LAST], p1[LAST]]

        def scores(t):
            width = BANK // 2 if t == 0 else BANK
            for b in range(T // width):
                cols = slice(b * width, (b + 1) * width)
                acc = psum.tile([P, BANK], F32, name="bank%d" % (len(banks) % BANKS))
                banks[t, b] = acc
                nc.tensor.matmul_mx(out=acc[:, 0:width], lhsT=q_codes[:, t * P:(t + 1) * P].bitcast(FP8X4),
                                    lhsT_scale=q_scales[:, t * P:(t + 1) * P],
                                    rhs=k_codes[:, cols].bitcast(FP8X4), rhs_scale=k_scales[:, cols],
                                    start=True, stop=True)
                if t == 0 and b % 2 == 1:
                    nc.vector.tensor_copy(out=a[t][:, cols], in_=acc[:, 0:width])
                else:
                    nc.scalar.copy(out=a[t][:, cols], in_=acc[:, 0:width])

        def pick_first(t):
            if t == 0:
                nc.vector.tensor_copy(p1[t][:, halves[0]], a[t][:].indirect(pick1[:, list_halves[0]]))
                nc.scalar.activation(p1[t][:, halves[1]], a[t][:].indirect(pick1[:, list_halves[1]]), COPY)
            else:
                nc.scalar.activation(p1[t][:], a[t][:].indirect(pick1[:]), COPY)

        def pick_second(t):
            nc.scalar.activation(p2[t][:], a[t][:].indirect(pick2[:]), COPY)

        def add_side(t):
            nc.vector.tensor_copy(f1[:].indirect(put1[:]), p1[t][:])
            nc.gpsimd.tensor_tensor(c1[t][:], a[t][:], f1[:], ALU.add)

        def subtract_side(t):
            nc.vector.tensor_copy(f2[:].indirect(put2[:]), p2[t][:])
            if t < LAST:
                nc.gpsimd.tensor_tensor(c2[t][:], a[t][:], f2[:], ALU.subtract)
            else:
                nc.vector.tensor_tensor(c2[t][:, 0:BANK], banks[t, 0][:], f2[:, 0:BANK], ALU.subtract)
                nc.vector.tensor_tensor(c2[t][:, BANK:SPLIT], banks[t, 1][:, 0:SPLIT - BANK], f2[:, BANK:SPLIT],
                                        ALU.subtract)
                nc.gpsimd.tensor_tensor(c2[t][:, SPLIT:], a[t][:, SPLIT:], f2[:, SPLIT:], ALU.subtract)

        def look_first(t):
            nc.scalar.activation(g1[t][:], c1[t][:].indirect(look1[:]), COPY)

        def look_second(t):
            nc.scalar.activation(g2[t][:], c2[t][:].indirect(look2[:]), COPY)

        def take_larger(t):
            parts = halves if t == LAST else [slice(0, I)]
            for cols in parts:
                nc.vector.tensor_tensor(larger[t][:, cols], g1[t][:, cols], g2[t][:, cols], ALU.max)

        def weave(t):
            for h in range(2):
                if t >= PACK // 2:
                    nc.vector.tensor_scalar(out=woven[h][:, :, t], in0=larger[t][:, halves[h]],
                                            scalar1=factor[:, t:t + 1], scalar2=None, op0=ALU.mult)
                else:
                    nc.scalar.activation(woven[h][:, :, t], larger[t][:, halves[h]], COPY, scale=factor[:, t:t + 1])

        def mix_half(h):
            g_codes = keep.tile([P, HALF], U32, name="g_codes%d" % h, align_bytes=64)
            g_scales = keep.tile([P, HALF], U8, name="g_scales%d" % h, align_bytes=64)
            nc.vector.quantize_mx(out=g_codes[:].bitcast(FP8X4), scales=g_scales[:],
                                  in_=woven[h][:].rearrange("p i t -> p (i t)"))
            for c in range(E // P):
                res = keep.tile([P, HALF], F32, name="res%d_%d" % (h, c))
                acc = psum.tile([P, BANK], F32, name="bank%d" % (FIRST_OUT_BANK + 2 * h + c))
                nc.tensor.matmul_mx(out=acc[:, 0:HALF], lhsT=m_codes[:, 2 * P * c:2 * P * (c + 1)].bitcast(FP4X4),
                                    lhsT_scale=m_scales[:, P * c:P * (c + 1)],
                                    rhs=g_codes[:].bitcast(FP8X4), rhs_scale=g_scales[:],
                                    start=True, stop=True)
                if h == 1 and c == 1:
                    nc.vector.tensor_copy(out=res[:], in_=acc[:, 0:HALF])
                else:
                    nc.scalar.copy(out=res[:], in_=acc[:, 0:HALF])
                queue = nc.scalar if (h == 1 and c == 0) else nc.sync
                queue.dma_start(out=out[c * P:(c + 1) * P, halves[h]], in_=res[:])

        for t in range(2):
            scores(t)
            pick_first(t)
            pick_second(t)
            add_side(t)
            subtract_side(t)
        scores(2)
        look_first(0)
        look_second(0)
        take_larger(0)
        pick_first(2)
        pick_second(2)
        scores(3)
        add_side(2)
        subtract_side(2)
        look_first(1)
        weave(0)
        look_second(1)
        take_larger(1)
        pick_first(3)
        pick_second(3)
        add_side(3)
        subtract_side(3)
        look_first(2)
        weave(1)
        look_second(2)
        take_larger(2)
        weave(2)
        look_first(3)
        look_second(3)
        take_larger(3)
        weave(3)
        for h in range(2):
            mix_half(h)
